import numpy as np
import ml_dtypes


def mxq(x, axis, fmt="e4m3"):
    dtype, down = {"e4m3": (ml_dtypes.float8_e4m3fn, 7), "e5m2": (ml_dtypes.float8_e5m2, 14)}[fmt]
    v = np.moveaxis(np.asarray(x, np.float32).astype(ml_dtypes.bfloat16).astype(np.float64), axis, -1)
    blocks = v.reshape(v.shape[:-1] + (-1, 32))
    amax = np.abs(blocks).max(-1, keepdims=True)
    byte = np.maximum(np.where(amax > 0, np.frexp(amax)[1] - 1 + 127, 0) - down, 1)
    scale = np.exp2(byte - 127.0)
    codes = (blocks / scale).astype(np.float32).astype(dtype).astype(np.float64)
    return np.moveaxis((codes * scale).reshape(v.shape), -1, axis)


WIDE = False


def mx_kscale(k):
    if not WIDE:
        return np.ones(k)
    levels = np.array([10, -10, 5, -5, 0])
    if k % 512:
        return np.exp2(np.random.permutation(np.resize(levels, k // 32))).repeat(32)
    a = np.empty((k // 512, 16))
    for p in range(k // 512):
        a[p, :8] = np.random.permutation(np.resize(levels, 8))
        for g in range(8):
            far = levels[np.abs(levels - a[p, g]) >= 10]
            a[p, g + 8] = far[np.random.randint(len(far))]
    return np.exp2(a.ravel()).repeat(32)


def f64(x):
    return np.asarray(x).astype(np.float64)


def striped(idx):
    return np.tile(np.asarray(idx).reshape(-1, 16).T, (8, 1)).astype(np.uint16)


def unstriped(offs):
    return offs[:16].T.reshape(-1).astype(np.int64)


def striped8(idx):
    return np.asarray(idx).reshape(8, -1, 16).transpose(0, 2, 1).reshape(128, -1).astype(np.uint16)


def unstriped8(offs):
    return offs.reshape(8, 16, -1).transpose(0, 2, 1).reshape(8, -1).astype(np.int64)


def pick8(x, idx, run):
    r = np.arange(len(x))
    return x[r[:, None], idx[r % (8 * run) // run]]


E2M1 = np.array([0.0, 0.5, 1.0, 1.5, 2.0, 3.0, 4.0, 6.0, -0.0, -0.5, -1.0, -1.5, -2.0, -3.0, -4.0, -6.0])


def pack_weight(w, fmt):
    k, n = w.shape
    w = f64(np.asarray(w, np.float32).astype(ml_dtypes.bfloat16)).reshape(k // 32, 32, n)
    amax = np.abs(w).max(1)
    if fmt == "e4m3":
        byte = np.frexp(amax)[1] - 1 + 127 - 7
    else:
        mant, ex = np.frexp(amax / 6.0)
        byte = np.where(mant > 0.5, ex, ex - 1) + 127
    byte = np.clip(np.where(amax > 0, byte, 1), 1, 254)
    scaled = (w * np.exp2(127.0 - byte)[:, None, :]).reshape(k, n).astype(np.float32)
    by_word = np.ascontiguousarray(scaled.reshape(k // 512, 128, 4, n).transpose(0, 1, 3, 2))
    if fmt == "e4m3":
        words = by_word.astype(ml_dtypes.float8_e4m3fn).view(np.uint8)
    else:
        c = by_word.astype(ml_dtypes.float4_e2m1fn).view(np.uint8) & 0xF
        words = (c[..., 0::2] | (c[..., 1::2] << 4)).reshape(k // 512, 128, 2 * n)
    return np.ascontiguousarray(words), np.ascontiguousarray(byte.astype(np.uint8).reshape(k // 512, 16, n))


def unpack_weight(words, scales, fmt):
    g, _, n = scales.shape
    words = np.ascontiguousarray(words).reshape(g, 128, n, -1)
    if fmt == "e4m3":
        vals = words.view(ml_dtypes.float8_e4m3fn).astype(np.float64)
    else:
        nib = np.empty((g, 128, n, 4), np.uint8)
        nib[..., 0::2] = words & 0xF
        nib[..., 1::2] = words >> 4
        vals = E2M1[nib]
    vals = vals * np.repeat(np.exp2(scales.astype(np.float64) - 127.0), 8, axis=1)[..., None]
    return vals.transpose(0, 1, 3, 2).reshape(g * 512, n)


K, J, R, T, O, C, N, S, Z, U = 512, 512, 512, 1024, 256, 1024, 256, 512, 1024, 128


def setup_inputs():
    n = np.random.standard_normal
    idx = np.stack([np.random.permutation(T)[:J] for _ in range(8)])
    idx2 = np.stack([np.random.permutation(C)[:J] for _ in range(8)])
    idx3 = np.stack([np.random.permutation(C)[:O] for _ in range(8)])
    idx4 = np.stack([np.random.permutation(C)[:O] for _ in range(8)])
    idx5 = np.random.permutation(Z)[:O]
    idx6 = np.stack([np.random.permutation(O)[:U] for _ in range(8)])
    idx7 = np.random.permutation(O)[:U]
    fk = mx_kscale(K)
    fr = mx_kscale(R)
    fs = mx_kscale(S)
    wp = pack_weight(n((K, R)) * 1 / np.sqrt(K) / fk[:, None] * fr, "e2m1")
    wbp = pack_weight(n((R, N)) * 1 / np.sqrt(R) / fr[:, None], "e4m3")
    xrp = pack_weight(n((S, Z)) / fs[:, None], "e4m3")
    wsp = pack_weight(n((S, N)) * 1 / np.sqrt(S) * fs[:, None], "e2m1")
    return {
        "ta": (np.random.randint(-7, 8, (K, T)).astype(np.float64)).astype(np.float32),
        "ga": ((np.random.randint(8, 25, (K, 1)) / 64.0) * fk[:, None]).astype(np.float32),
        "w_words": wp[0],
        "w_scales": wp[1],
        "sa": (np.random.uniform(0.5, 1.6, (R, 1))).astype(np.float32),
        "sb": (np.random.uniform(0.5, 1.6, (R, 1))).astype(np.float32),
        "wb_words": wbp[0],
        "wb_scales": wbp[1],
        "xr_words": xrp[0],
        "xr_scales": xrp[1],
        "ws_words": wsp[0],
        "ws_scales": wsp[1],
        "so": (np.random.uniform(0.5, 1.6, (N, 1))).astype(np.float32),
        "sp": (np.random.uniform(0.5, 1.6, (N, 1))).astype(np.float32),
        "offs": striped8(idx),
        "offs2": striped8(idx2),
        "offs3": striped8(idx3),
        "offs4": striped8(idx4),
        "offs5": striped(idx5),
        "offs6": striped8(idx6),
        "offs7": striped(idx7),
    }


def reference(ta, ga, w_words, w_scales, sa, sb, wb_words, wb_scales, xr_words, xr_scales, ws_words, ws_scales, so, sp, offs, offs2, offs3, offs4, offs5, offs6, offs7):
    idx = unstriped8(offs)
    idx2 = unstriped8(offs2)
    idx3 = unstriped8(offs3)
    idx4 = unstriped8(offs4)
    idx5 = unstriped(offs5)
    idx6 = unstriped8(offs6)
    idx7 = unstriped(offs7)
    wu = unpack_weight(w_words, w_scales, "e2m1")
    wbu = unpack_weight(wb_words, wb_scales, "e4m3")
    xru = unpack_weight(xr_words, xr_scales, "e4m3")
    wsu = unpack_weight(ws_words, ws_scales, "e2m1")
    xc = pick8(f64(ta), idx, 64) * f64(ga)
    xcq = mxq(xc, 0, "e4m3")
    a = wu.T @ xcq
    pw = np.zeros((R, C))
    pw[np.arange(R)[:, None], idx2[np.arange(R) % 512 // 64]] = a
    hid = np.abs(pick8(pw, idx3, 64) * f64(sa) - pick8(pw, idx4, 64) * f64(sb))
    hidq = mxq(hid, 0, "e4m3")
    xridx5g = xru[:, idx5]
    p = wbu.T @ hidq + wsu.T @ xridx5g
    y = pick8(p, idx6, 16) * f64(so) - p[:, idx7] * f64(sp)
    return y

@@ -1,0 +1,269 @@
+from contextlib import ExitStack
+
+import concourse.mybir as mybir
+
+K, J, R, T, O, C, N, S, Z, U = 512, 512, 512, 1024, 256, 1024, 256, 512, 1024, 128
+FLOPS = 2 * K * R * J + 2 * R * N * O + 2 * S * N * O
+
+F32 = mybir.dt.float32
+BF16 = mybir.dt.bfloat16
+I32 = mybir.dt.int32
+U32 = mybir.dt.uint32
+U16 = mybir.dt.uint16
+U8 = mybir.dt.uint8
+FP8X4 = mybir.dt.float8_e4m3fn_x4
+FP4X4 = mybir.dt.float4_e2m1fn_x4
+COPY = mybir.ActivationFunctionType.Copy
+ABS = mybir.ActivationFunctionType.Abs
+SUB = mybir.AluOpType.subtract
+
+P = 128
+PACK = 4
+H = J // 2
+Q = J // 4
+V = O // 2
+
+
+def tile_picked_codes_plain_one_boardpair_reminder_onepair_kernel(
+    tc, ta, ga, w_words, w_scales, sa, sb, wb_words, wb_scales, xr_words, xr_scales, ws_words, ws_scales,
+    so, sp, offs, offs2, offs3, offs4, offs5, offs6, offs7, out,
+):
+    nc = tc.nc
+    with ExitStack() as ctx:
+        lists = ctx.enter_context(tc.tile_pool(name="lists", bufs=1))
+        keep = ctx.enter_context(tc.tile_pool(name="keep", bufs=1))
+        shared = ctx.enter_context(tc.tile_pool(name="shared", bufs=1))
+        psum = ctx.enter_context(tc.psum_pool(name="psum", bufs=1))
+
+        def load_list(src, name):
+            tile = lists.tile(list(src.shape), U16, name=name)
+            nc.sync.dma_start(tile[:], src)
+            return tile
+
+        def load_column(src, name, pattern, **sizes):
+            view = src.rearrange(pattern, **sizes)
+            tile = keep.tile(list(view.shape), F32, name=name)
+            with nc.allow_non_contiguous_dma(reason="one value a row"):
+                nc.sync.dma_start(tile[:], view)
+            return tile
+
+        def zeroed_plane(width, name):
+            tile = keep.tile([P, width], U8, name=name, align_bytes=64)
+            nc.vector.memset(tile[:].bitcast(I32), 0)
+            return tile
+
+        def load_plane(tile, src):
+            for q in range(4):
+                nc.sync.dma_start(tile[32 * q : 32 * q + 4, :].bitcast(I32), src[0, 4 * q : 4 * q + 4, :].bitcast(I32))
+
+        warm = keep.tile([P, 16], F32, name="warm")
+        nc.vector.memset(warm[:, 0:8], 0.0)
+        nc.scalar.activation(out=warm[:, 8:16], in_=warm[:, 0:8], func=COPY)
+        w_spread = zeroed_plane(R, "w_spread")
+        xr_plane = zeroed_plane(Z, "xr_plane")
+        wb_plane = zeroed_plane(N, "wb_plane")
+        ws_plane = zeroed_plane(N, "ws_plane")
+        pw = [keep.tile([P, C], F32, name=f"pw{t}") for t in range(PACK)]
+        for t in range(PACK):
+            nc.vector.memset(pw[t][:], 0.0)
+
+        ta_rows = ta.rearrange("(p t) c -> p t c", t=PACK)
+        ta_sb = [keep.tile([P, T], F32, name=f"ta{t}") for t in range(PACK)]
+        nc.sync.dma_start(ta_sb[0][:], ta_rows[:, 0, :])
+        l1 = load_list(offs, "l1")
+        ga_sb = load_column(ga, "ga_sb", "(p t) o -> p (t o)", t=PACK)
+        w_raw = keep.tile([P, 2 * R], U8, name="w_raw")
+        nc.sync.dma_start(w_raw[:].bitcast(I32), w_words[0].bitcast(I32))
+        w_stage = keep.tile([4, 4, R // 4], I32, name="w_stage")
+        nc.sync.dma_start(w_stage[:], w_scales[0].bitcast(I32).rearrange("(q r) n -> r q n", r=4))
+        for t in range(1, PACK):
+            nc.sync.dma_start(ta_sb[t][:], ta_rows[:, t, :])
+        l2 = load_list(offs2, "l2")
+        l3 = load_list(offs3, "l3")
+        l4 = load_list(offs4, "l4")
+        sa_sb = load_column(sa, "sa_sb", "(p t) o -> p (t o)", t=PACK)
+        sb_sb = load_column(sb, "sb_sb", "(p t) o -> p (t o)", t=PACK)
+        xr_sb = keep.tile([P, Z], U32, name="xr_sb")
+        nc.sync.dma_start(xr_sb[:].bitcast(I32), xr_words[0].rearrange("p n t -> p (n t)").bitcast(I32))
+        l5 = load_list(offs5, "l5")
+        load_plane(xr_plane, xr_scales)
+        ws_sb = keep.tile([P, 2 * N], U8, name="ws_sb", align_bytes=64)
+        nc.sync.dma_start(ws_sb[:].bitcast(I32), ws_words[0].bitcast(I32))
+        load_plane(ws_plane, ws_scales)
+        wb_sb = keep.tile([P, N], U32, name="wb_sb", align_bytes=64)
+        nc.sync.dma_start(wb_sb[:].bitcast(I32), wb_words[0].rearrange("p n t -> p (n t)").bitcast(I32))
+        load_plane(wb_plane, wb_scales)
+        l6 = load_list(offs6, "l6")
+        l7 = load_list(offs7, "l7")
+        so_sb = load_column(so, "so_sb", "(i p) o -> p (i o)", p=P)
+        sp_sb = load_column(sp, "sp_sb", "(i p) o -> p (i o)", p=P)
+
+        for q in range(4):
+            nc.vector.tensor_copy(w_spread[32 * q : 32 * q + 4, :].bitcast(I32), w_stage[:, q, :])
+        w_dealt = keep.tile([P, 2 * R], U8, name="w_dealt", align_bytes=64)
+        nc.vector.tensor_copy(
+            w_dealt[:].rearrange("p (t m b) -> p t m b", t=PACK, b=2),
+            w_raw[:].rearrange("p (m t b) -> p t m b", t=PACK, b=2),
+        )
+        w_plane = keep.tile([P, R], U8, name="w_plane", align_bytes=64)
+        nc.vector.tensor_copy(
+            w_plane[:].rearrange("p (t m) -> p t m", t=PACK),
+            w_spread[:].rearrange("p (m t) -> p t m", t=PACK),
+        )
+
+        xg = shared.tile([P, 10, H], BF16, name="xg", offset=2048, align_bytes=64)
+        xflat = xg[:].rearrange("p b c -> p (b c)")
+
+        def fetch_ta(t, first, count, block):
+            nc.scalar.activation(
+                out=xflat[:, block * H : block * H + count],
+                in_=ta_sb[t][:].indirect(l1[:, first // 16 : (first + count) // 16]),
+                func=COPY,
+                scale=ga_sb[:, t : t + 1],
+            )
+
+        x_il = [keep.tile([P, H * PACK], BF16, name=f"x_il{h}", align_bytes=64) for h in range(2)]
+        x_codes = keep.tile([P, J], U32, name="x_codes", align_bytes=64)
+        x_plane = keep.tile([P, J], U8, name="x_plane", align_bytes=64)
+
+        def quantise_x(first, count, src):
+            cols = slice(first, first + count)
+            nc.vector.quantize_mx(out=x_codes[:, cols].bitcast(FP8X4), scales=x_plane[:, cols], in_=src)
+
+        def first_product(t, first, count, name):
+            acc = psum.tile([P, count], F32, name=name, tag=name)
+            cols = slice(first, first + count)
+            nc.tensor.matmul_mx(
+                out=acc[:],
+                lhsT=w_dealt[:, 2 * P * t : 2 * P * (t + 1)].bitcast(FP4X4),
+                lhsT_scale=w_plane[:, P * t : P * (t + 1)],
+                rhs=x_codes[:, cols].bitcast(FP8X4),
+                rhs_scale=x_plane[:, cols],
+                start=True,
+                stop=True,
+            )
+            return acc
+
+        def scatter(t, first, count, src):
+            nc.vector.tensor_copy(pw[t][:].indirect(l2[:, first // 16 : (first + count) // 16]), src[:])
+
+        fetch_ta(0, 0, J, 0)
+        fetch_ta(1, 0, J, 2)
+        fetch_ta(2, 0, H, 4)
+        fetch_ta(3, 0, H, 6)
+        for q in range(2):
+            nc.vector.tensor_copy(
+                x_il[0][:, q * Q * PACK : (q + 1) * Q * PACK].rearrange("p (c i t) -> p c t i", i=4, t=PACK),
+                xg[:, 0:8:2, q * Q : (q + 1) * Q].rearrange("p t (c i) -> p c t i", i=4),
+            )
+        for q in range(2):
+            quantise_x(q * Q, Q, x_il[0][:, q * Q * PACK : (q + 1) * Q * PACK])
+        early = [first_product(0, q * Q, Q, f"bank{q}") for q in range(2)]
+        acc10 = first_product(1, 0, H, "bank2")
+        a0q = [keep.tile([P, Q], F32, name=f"a0q{q}") for q in range(2)]
+        for q in range(2):
+            nc.vector.tensor_copy(a0q[q][:], early[q][:])
+        for q in range(2):
+            scatter(0, q * Q, Q, a0q[q])
+
+        fetch_ta(3, H, H, 8)
+        fetch_ta(2, H, H, 6)
+        nc.scalar.copy(
+            x_il[1][:].rearrange("p (c u v) -> p c u v", u=2, v=2),
+            xg[:].rearrange("p (u b) c -> p c u b", u=2)[:, :, :, 1:4:2],
+        )
+        quantise_x(H, H, x_il[1][:])
+        a10 = shared.tile([P, H], F32, name="a10", offset=2048, align_bytes=64)
+        nc.scalar.copy(a10[:], acc10[:])
+        scatter(1, 0, H, a10)
+        for t in range(2):
+            acc = first_product(t, H, H, f"bank{3 + t}")
+            half = keep.tile([P, H], F32, name=f"a{t}1")
+            nc.scalar.copy(half[:], acc[:])
+            scatter(t, H, H, half)
+        acc2 = first_product(2, 0, J, "bank5")
+        a2 = keep.tile([P, J], F32, name="a2")
+        nc.scalar.copy(a2[:], acc2[:])
+        scatter(2, 0, J, a2)
+        acc3 = first_product(3, 0, J, "bank6")
+        a3 = shared.tile([P, J], F32, name="a3", offset=0, align_bytes=64)
+        nc.scalar.copy(a3[:], acc3[:])
+        scatter(3, 0, J, a3)
+
+        g3 = keep.tile([P, 3, O], F32, name="g3")
+        g4 = keep.tile([P, 3, O], F32, name="g4")
+        diff = keep.tile([P, PACK, O], F32, name="diff")
+        h_il = keep.tile([P, O, PACK], BF16, name="h_il", align_bytes=64)
+
+        def fetch_pw(t, first_out, second_out):
+            nc.scalar.activation(out=first_out, in_=pw[t][:].indirect(l3[:]), func=COPY, scale=sa_sb[:, t : t + 1])
+            nc.scalar.activation(out=second_out, in_=pw[t][:].indirect(l4[:]), func=COPY, scale=sb_sb[:, t : t + 1])
+
+        def magnitude(t, cols):
+            nc.scalar.activation(
+                out=h_il[:, cols, t : t + 2], in_=diff[:, t : t + 2, cols].rearrange("p t o -> p o t"), func=ABS
+            )
+
+        for t in range(2):
+            fetch_pw(t, g3[:, t, :], g4[:, t, :])
+        nc.gpsimd.tensor_tensor(diff[:, 0:2, :], g3[:, 0:2, :], g4[:, 0:2, :], SUB)
+        magnitude(0, slice(0, O))
+        fetch_pw(2, g3[:, 2, :], g4[:, 2, :])
+        nc.gpsimd.tensor_tensor(diff[:, 2, :], g3[:, 2, :], g4[:, 2, :], SUB)
+        fetch_pw(3, diff[:, 0, :], diff[:, 1, :])
+
+        xr_codes = shared.tile([P, O], U32, name="xr_codes", offset=0, align_bytes=64)
+        xr_picked = shared.tile([P, O], U8, name="xr_picked", offset=4 * O, align_bytes=64)
+        nc.vector.tensor_copy(xr_codes[:], xr_sb[:].indirect(l5[:]))
+        nc.vector.tensor_copy(xr_picked[:], xr_plane[:].indirect(l5[:]))
+        halves = [slice(v * V, (v + 1) * V) for v in range(2)]
+        p_acc = {}
+        for v in range(2):
+            for i in range(2):
+                p_acc[i, v] = psum.tile([P, V], F32, name=f"p_acc{i}{v}", tag=f"bank{2 * v + i}")
+                nc.tensor.matmul_mx(
+                    out=p_acc[i, v][:],
+                    lhsT=ws_sb[:, 2 * P * i : 2 * P * (i + 1)].bitcast(FP4X4),
+                    lhsT_scale=ws_plane[:, P * i : P * (i + 1)],
+                    rhs=xr_codes[:, halves[v]].bitcast(FP8X4),
+                    rhs_scale=xr_picked[:, halves[v]],
+                    start=True,
+                    stop=False,
+                )
+
+        h_codes = keep.tile([P, O], U32, name="h_codes", align_bytes=64)
+        h_plane = keep.tile([P, O], U8, name="h_plane", align_bytes=64)
+        p_sb = [keep.tile([P, O], F32, name=f"p_sb{i}") for i in range(2)]
+        for v in range(2):
+            nc.vector.tensor_tensor(diff[:, 3, halves[v]], diff[:, 0, halves[v]], diff[:, 1, halves[v]], SUB)
+        for v in range(2):
+            magnitude(2, halves[v])
+        for v in range(2):
+            nc.vector.quantize_mx(
+                out=h_codes[:, halves[v]].bitcast(FP8X4),
+                scales=h_plane[:, halves[v]],
+                in_=h_il[:, halves[v], :].rearrange("p o t -> p (o t)"),
+            )
+        for v in range(2):
+            for i in range(2):
+                nc.tensor.matmul_mx(
+                    out=p_acc[i, v][:],
+                    lhsT=wb_sb[:, P * i : P * (i + 1)].bitcast(FP8X4),
+                    lhsT_scale=wb_plane[:, P * i : P * (i + 1)],
+                    rhs=h_codes[:, halves[v]].bitcast(FP8X4),
+                    rhs_scale=h_plane[:, halves[v]],
+                    start=False,
+                    stop=True,
+                )
+        for i in range(2):
+            nc.scalar.copy(p_sb[i][:, halves[0]], p_acc[i, 0][:])
+        for i in range(2):
+            nc.vector.tensor_copy(p_sb[i][:, halves[1]], p_acc[i, 1][:])
+        for i in range(2):
+            first = keep.tile([P, U], F32, name=f"first{i}")
+            second = keep.tile([P, U], F32, name=f"second{i}")
+            nc.scalar.activation(out=first[:], in_=p_sb[i][:].indirect(l6[:]), func=COPY, scale=so_sb[:, i : i + 1])
+            nc.scalar.activation(out=second[:], in_=p_sb[i][:].indirect(l7[:]), func=COPY, scale=sp_sb[:, i : i + 1])
+            res = keep.tile([P, U], F32, name=f"res{i}")
+            nc.vector.tensor_tensor(res[:], first[:], second[:], SUB)
+            nc.sync.dma_start(out[P * i : P * (i + 1), :], res[:])

@@ -40,11 +40,11 @@ def tile_picked_codes_plain_one_boardpair_reminder_onepair_kernel(
             nc.sync.dma_start(tile[:], src)
             return tile
 
-        def load_column(src, name, pattern, **sizes):
+        def load_column(queue, src, name, pattern, **sizes):
             view = src.rearrange(pattern, **sizes)
             tile = keep.tile(list(view.shape), F32, name=name)
             with nc.allow_non_contiguous_dma(reason="one value a row"):
-                nc.sync.dma_start(tile[:], view)
+                queue.dma_start(tile[:], view)
             return tile
 
         def zeroed_plane(width, name):
@@ -71,18 +71,18 @@ def tile_picked_codes_plain_one_boardpair_reminder_onepair_kernel(
         ta_sb = [keep.tile([P, T], F32, name=f"ta{t}") for t in range(PACK)]
         nc.sync.dma_start(ta_sb[0][:], ta_rows[:, 0, :])
         l1 = load_list(offs, "l1")
-        ga_sb = load_column(ga, "ga_sb", "(p t) o -> p (t o)", t=PACK)
+        ga_sb = load_column(nc.scalar, ga, "ga_sb", "(p t) o -> p (t o)", t=PACK)
         w_raw = keep.tile([P, 2 * R], U8, name="w_raw")
-        nc.sync.dma_start(w_raw[:].bitcast(I32), w_words[0].bitcast(I32))
+        nc.scalar.dma_start(w_raw[:].bitcast(I32), w_words[0].bitcast(I32))
         w_stage = keep.tile([4, 4, R // 4], I32, name="w_stage")
-        nc.sync.dma_start(w_stage[:], w_scales[0].bitcast(I32).rearrange("(q r) n -> r q n", r=4))
+        nc.scalar.dma_start(w_stage[:], w_scales[0].bitcast(I32).rearrange("(q r) n -> r q n", r=4))
         for t in range(1, PACK):
             nc.sync.dma_start(ta_sb[t][:], ta_rows[:, t, :])
         l2 = load_list(offs2, "l2")
         l3 = load_list(offs3, "l3")
         l4 = load_list(offs4, "l4")
-        sa_sb = load_column(sa, "sa_sb", "(p t) o -> p (t o)", t=PACK)
-        sb_sb = load_column(sb, "sb_sb", "(p t) o -> p (t o)", t=PACK)
+        sa_sb = load_column(nc.sync, sa, "sa_sb", "(p t) o -> p (t o)", t=PACK)
+        sb_sb = load_column(nc.sync, sb, "sb_sb", "(p t) o -> p (t o)", t=PACK)
         xr_sb = keep.tile([P, Z], U32, name="xr_sb")
         nc.sync.dma_start(xr_sb[:].bitcast(I32), xr_words[0].rearrange("p n t -> p (n t)").bitcast(I32))
         l5 = load_list(offs5, "l5")
@@ -95,8 +95,8 @@ def tile_picked_codes_plain_one_boardpair_reminder_onepair_kernel(
         load_plane(wb_plane, wb_scales)
         l6 = load_list(offs6, "l6")
         l7 = load_list(offs7, "l7")
-        so_sb = load_column(so, "so_sb", "(i p) o -> p (i o)", p=P)
-        sp_sb = load_column(sp, "sp_sb", "(i p) o -> p (i o)", p=P)
+        so_sb = load_column(nc.sync, so, "so_sb", "(i p) o -> p (i o)", p=P)
+        sp_sb = load_column(nc.sync, sp, "sp_sb", "(i p) o -> p (i o)", p=P)
 
         for q in range(4):
             nc.vector.tensor_copy(w_spread[32 * q : 32 * q + 4, :].bitcast(I32), w_stage[:, q, :])
@@ -111,7 +111,7 @@ def tile_picked_codes_plain_one_boardpair_reminder_onepair_kernel(
             w_spread[:].rearrange("p (m t) -> p t m", t=PACK),
         )
 
-        xg = shared.tile([P, 10, H], BF16, name="xg", offset=2048, align_bytes=64)
+        xg = shared.tile([P, 9, H], BF16, name="xg", offset=2048, align_bytes=64)
         xflat = xg[:].rearrange("p b c -> p (b c)")
 
         def fetch_ta(t, first, count, block):
@@ -122,13 +122,17 @@ def tile_picked_codes_plain_one_boardpair_reminder_onepair_kernel(
                 scale=ga_sb[:, t : t + 1],
             )
 
-        x_il = [keep.tile([P, H * PACK], BF16, name=f"x_il{h}", align_bytes=64) for h in range(2)]
+        x_il = keep.tile([P, J, PACK], BF16, name="x_il", align_bytes=64)
         x_codes = keep.tile([P, J], U32, name="x_codes", align_bytes=64)
         x_plane = keep.tile([P, J], U8, name="x_plane", align_bytes=64)
 
-        def quantise_x(first, count, src):
+        def quantise_x(first, count):
             cols = slice(first, first + count)
-            nc.vector.quantize_mx(out=x_codes[:, cols].bitcast(FP8X4), scales=x_plane[:, cols], in_=src)
+            nc.vector.quantize_mx(
+                out=x_codes[:, cols].bitcast(FP8X4),
+                scales=x_plane[:, cols],
+                in_=x_il[:, cols, :].rearrange("p c t -> p (c t)"),
+            )
 
         def first_product(t, first, count, name):
             acc = psum.tile([P, count], F32, name=name, tag=name)
@@ -149,15 +153,14 @@ def tile_picked_codes_plain_one_boardpair_reminder_onepair_kernel(
 
         fetch_ta(0, 0, J, 0)
         fetch_ta(1, 0, J, 2)
+        nc.vector.tensor_copy(x_il[:, :, 0:2], xflat[:, 0 : 2 * J].rearrange("p (t c) -> p c t", t=2))
         fetch_ta(2, 0, H, 4)
+        nc.vector.tensor_copy(x_il[:, 0:H, 2], xg[:, 4, :])
         fetch_ta(3, 0, H, 6)
         for q in range(2):
-            nc.vector.tensor_copy(
-                x_il[0][:, q * Q * PACK : (q + 1) * Q * PACK].rearrange("p (c i t) -> p c t i", i=4, t=PACK),
-                xg[:, 0:8:2, q * Q : (q + 1) * Q].rearrange("p t (c i) -> p c t i", i=4),
-            )
+            nc.vector.tensor_copy(x_il[:, q * Q : (q + 1) * Q, 3], xg[:, 6, q * Q : (q + 1) * Q])
         for q in range(2):
-            quantise_x(q * Q, Q, x_il[0][:, q * Q * PACK : (q + 1) * Q * PACK])
+            quantise_x(q * Q, Q)
         early = [first_product(0, q * Q, Q, f"bank{q}") for q in range(2)]
         acc10 = first_product(1, 0, H, "bank2")
         a0q = [keep.tile([P, Q], F32, name=f"a0q{q}") for q in range(2)]
@@ -168,11 +171,8 @@ def tile_picked_codes_plain_one_boardpair_reminder_onepair_kernel(
 
         fetch_ta(3, H, H, 8)
         fetch_ta(2, H, H, 6)
-        nc.scalar.copy(
-            x_il[1][:].rearrange("p (c u v) -> p c u v", u=2, v=2),
-            xg[:].rearrange("p (u b) c -> p c u b", u=2)[:, :, :, 1:4:2],
-        )
-        quantise_x(H, H, x_il[1][:])
+        nc.scalar.copy(x_il[:, H:J, 2:4], xg[:, 6:9:2, :].rearrange("p t c -> p c t"))
+        quantise_x(H, H)
         a10 = shared.tile([P, H], F32, name="a10", offset=2048, align_bytes=64)
         nc.scalar.copy(a10[:], acc10[:])
         scatter(1, 0, H, a10)

@@ -65,17 +65,17 @@ def tile_picked_codes_plain_one_boardpair_reminder_onepair_kernel(
         ws_plane = zeroed_plane(N, "ws_plane")
         pw = [keep.tile([P, C], F32, name=f"pw{t}") for t in range(PACK)]
         for t in range(PACK):
-            nc.vector.memset(pw[t][:], 0.0)
+            (nc.vector if t < 2 else nc.gpsimd).memset(pw[t][:], 0.0)
 
         ta_rows = ta.rearrange("(p t) c -> p t c", t=PACK)
         ta_sb = [keep.tile([P, T], F32, name=f"ta{t}") for t in range(PACK)]
+        w_raw = keep.tile([P, 2 * R], U8, name="w_raw")
+        nc.sync.dma_start(w_raw[:].bitcast(I32), w_words[0].bitcast(I32))
         nc.sync.dma_start(ta_sb[0][:], ta_rows[:, 0, :])
         l1 = load_list(offs, "l1")
-        ga_sb = load_column(nc.scalar, ga, "ga_sb", "(p t) o -> p (t o)", t=PACK)
-        w_raw = keep.tile([P, 2 * R], U8, name="w_raw")
-        nc.scalar.dma_start(w_raw[:].bitcast(I32), w_words[0].bitcast(I32))
+        ga_sb = load_column(nc.sync, ga, "ga_sb", "(p t) o -> p (t o)", t=PACK)
         w_stage = keep.tile([4, 4, R // 4], I32, name="w_stage")
-        nc.scalar.dma_start(w_stage[:], w_scales[0].bitcast(I32).rearrange("(q r) n -> r q n", r=4))
+        nc.sync.dma_start(w_stage[:], w_scales[0].bitcast(I32).rearrange("(q r) n -> r q n", r=4))
         for t in range(1, PACK):
             nc.sync.dma_start(ta_sb[t][:], ta_rows[:, t, :])
         l2 = load_list(offs2, "l2")

from contextlib import ExitStack

import concourse.mybir as mybir

K, J, R, T, O, C, N, S, Z, U = 512, 512, 512, 1024, 256, 1024, 256, 512, 1024, 128
FLOPS = 2 * K * R * J + 2 * R * N * O + 2 * S * N * O

F32 = mybir.dt.float32
BF16 = mybir.dt.bfloat16
I32 = mybir.dt.int32
U32 = mybir.dt.uint32
U16 = mybir.dt.uint16
U8 = mybir.dt.uint8
FP8X4 = mybir.dt.float8_e4m3fn_x4
FP4X4 = mybir.dt.float4_e2m1fn_x4
COPY = mybir.ActivationFunctionType.Copy
ABS = mybir.ActivationFunctionType.Abs
SUB = mybir.AluOpType.subtract

P = 128
PACK = 4
H = J // 2
Q = J // 4
V = O // 2


def tile_picked_codes_plain_one_boardpair_reminder_onepair_kernel(
    tc, ta, ga, w_words, w_scales, sa, sb, wb_words, wb_scales, xr_words, xr_scales, ws_words, ws_scales,
    so, sp, offs, offs2, offs3, offs4, offs5, offs6, offs7, out,
):
    nc = tc.nc
    with ExitStack() as ctx:
        lists = ctx.enter_context(tc.tile_pool(name="lists", bufs=1))
        keep = ctx.enter_context(tc.tile_pool(name="keep", bufs=1))
        shared = ctx.enter_context(tc.tile_pool(name="shared", bufs=1))
        psum = ctx.enter_context(tc.psum_pool(name="psum", bufs=1))

        def load_list(src, name):
            tile = lists.tile(list(src.shape), U16, name=name)
            nc.sync.dma_start(tile[:], src)
            return tile

        def load_column(queue, src, name, pattern, **sizes):
            view = src.rearrange(pattern, **sizes)
            tile = keep.tile(list(view.shape), F32, name=name)
            with nc.allow_non_contiguous_dma(reason="one value a row"):
                queue.dma_start(tile[:], view)
            return tile

        def zeroed_plane(width, name):
            tile = keep.tile([P, width], U8, name=name, align_bytes=64)
            nc.vector.memset(tile[:].bitcast(I32), 0)
            return tile

        def load_plane(tile, src):
            for q in range(4):
                nc.sync.dma_start(tile[32 * q : 32 * q + 4, :].bitcast(I32), src[0, 4 * q : 4 * q + 4, :].bitcast(I32))

        warm = keep.tile([P, 16], F32, name="warm")
        nc.vector.memset(warm[:, 0:8], 0.0)
        nc.scalar.activation(out=warm[:, 8:16], in_=warm[:, 0:8], func=COPY)
        w_spread = zeroed_plane(R, "w_spread")
        xr_plane = zeroed_plane(Z, "xr_plane")
        wb_plane = zeroed_plane(N, "wb_plane")
        ws_plane = zeroed_plane(N, "ws_plane")
        pw = [keep.tile([P, C], F32, name=f"pw{t}") for t in range(PACK)]
        for t in range(PACK):
            (nc.vector if t < 2 else nc.gpsimd).memset(pw[t][:], 0.0)

        ta_rows = ta.rearrange("(p t) c -> p t c", t=PACK)
        ta_sb = [keep.tile([P, T], F32, name=f"ta{t}") for t in range(PACK)]
        w_raw = keep.tile([P, 2 * R], U8, name="w_raw")
        nc.sync.dma_start(w_raw[:].bitcast(I32), w_words[0].bitcast(I32))
        nc.sync.dma_start(ta_sb[0][:], ta_rows[:, 0, :])
        l1 = load_list(offs, "l1")
        ga_sb = load_column(nc.sync, ga, "ga_sb", "(p t) o -> p (t o)", t=PACK)
        w_stage = keep.tile([4, 4, R // 4], I32, name="w_stage")
        nc.sync.dma_start(w_stage[:], w_scales[0].bitcast(I32).rearrange("(q r) n -> r q n", r=4))
        for t in range(1, PACK):
            nc.sync.dma_start(ta_sb[t][:], ta_rows[:, t, :])
        l2 = load_list(offs2, "l2")
        l3 = load_list(offs3, "l3")
        l4 = load_list(offs4, "l4")
        sa_sb = load_column(nc.sync, sa, "sa_sb", "(p t) o -> p (t o)", t=PACK)
        sb_sb = load_column(nc.sync, sb, "sb_sb", "(p t) o -> p (t o)", t=PACK)
        xr_sb = keep.tile([P, Z], U32, name="xr_sb")
        nc.sync.dma_start(xr_sb[:].bitcast(I32), xr_words[0].rearrange("p n t -> p (n t)").bitcast(I32))
        l5 = load_list(offs5, "l5")
        load_plane(xr_plane, xr_scales)
        ws_sb = keep.tile([P, 2 * N], U8, name="ws_sb", align_bytes=64)
        nc.sync.dma_start(ws_sb[:].bitcast(I32), ws_words[0].bitcast(I32))
        load_plane(ws_plane, ws_scales)
        wb_sb = keep.tile([P, N], U32, name="wb_sb", align_bytes=64)
        nc.sync.dma_start(wb_sb[:].bitcast(I32), wb_words[0].rearrange("p n t -> p (n t)").bitcast(I32))
        load_plane(wb_plane, wb_scales)
        l6 = load_list(offs6, "l6")
        l7 = load_list(offs7, "l7")
        so_sb = load_column(nc.sync, so, "so_sb", "(i p) o -> p (i o)", p=P)
        sp_sb = load_column(nc.sync, sp, "sp_sb", "(i p) o -> p (i o)", p=P)

        for q in range(4):
            nc.vector.tensor_copy(w_spread[32 * q : 32 * q + 4, :].bitcast(I32), w_stage[:, q, :])
        w_dealt = keep.tile([P, 2 * R], U8, name="w_dealt", align_bytes=64)
        nc.vector.tensor_copy(
            w_dealt[:].rearrange("p (t m b) -> p t m b", t=PACK, b=2),
            w_raw[:].rearrange("p (m t b) -> p t m b", t=PACK, b=2),
        )
        w_plane = keep.tile([P, R], U8, name="w_plane", align_bytes=64)
        nc.vector.tensor_copy(
            w_plane[:].rearrange("p (t m) -> p t m", t=PACK),
            w_spread[:].rearrange("p (m t) -> p t m", t=PACK),
        )

        xg = shared.tile([P, 9, H], BF16, name="xg", offset=2048, align_bytes=64)
        xflat = xg[:].rearrange("p b c -> p (b c)")

        def fetch_ta(t, first, count, block):
            nc.scalar.activation(
                out=xflat[:, block * H : block * H + count],
                in_=ta_sb[t][:].indirect(l1[:, first // 16 : (first + count) // 16]),
                func=COPY,
                scale=ga_sb[:, t : t + 1],
            )

        x_il = keep.tile([P, J, PACK], BF16, name="x_il", align_bytes=64)
        x_codes = keep.tile([P, J], U32, name="x_codes", align_bytes=64)
        x_plane = keep.tile([P, J], U8, name="x_plane", align_bytes=64)

        def quantise_x(first, count):
            cols = slice(first, first + count)
            nc.vector.quantize_mx(
                out=x_codes[:, cols].bitcast(FP8X4),
                scales=x_plane[:, cols],
                in_=x_il[:, cols, :].rearrange("p c t -> p (c t)"),
            )

        def first_product(t, first, count, name):
            acc = psum.tile([P, count], F32, name=name, tag=name)
            cols = slice(first, first + count)
            nc.tensor.matmul_mx(
                out=acc[:],
                lhsT=w_dealt[:, 2 * P * t : 2 * P * (t + 1)].bitcast(FP4X4),
                lhsT_scale=w_plane[:, P * t : P * (t + 1)],
                rhs=x_codes[:, cols].bitcast(FP8X4),
                rhs_scale=x_plane[:, cols],
                start=True,
                stop=True,
            )
            return acc

        def scatter(t, first, count, src):
            nc.vector.tensor_copy(pw[t][:].indirect(l2[:, first // 16 : (first + count) // 16]), src[:])

        fetch_ta(0, 0, J, 0)
        fetch_ta(1, 0, J, 2)
        nc.vector.tensor_copy(x_il[:, :, 0:2], xflat[:, 0 : 2 * J].rearrange("p (t c) -> p c t", t=2))
        fetch_ta(2, 0, H, 4)
        nc.vector.tensor_copy(x_il[:, 0:H, 2], xg[:, 4, :])
        fetch_ta(3, 0, H, 6)
        for q in range(2):
            nc.vector.tensor_copy(x_il[:, q * Q : (q + 1) * Q, 3], xg[:, 6, q * Q : (q + 1) * Q])
        for q in range(2):
            quantise_x(q * Q, Q)
        early = [first_product(0, q * Q, Q, f"bank{q}") for q in range(2)]
        acc10 = first_product(1, 0, H, "bank2")
        a0q = [keep.tile([P, Q], F32, name=f"a0q{q}") for q in range(2)]
        for q in range(2):
            nc.vector.tensor_copy(a0q[q][:], early[q][:])
        for q in range(2):
            scatter(0, q * Q, Q, a0q[q])

        fetch_ta(3, H, H, 8)
        fetch_ta(2, H, H, 6)
        nc.scalar.copy(x_il[:, H:J, 2:4], xg[:, 6:9:2, :].rearrange("p t c -> p c t"))
        quantise_x(H, H)
        a10 = shared.tile([P, H], F32, name="a10", offset=2048, align_bytes=64)
        nc.scalar.copy(a10[:], acc10[:])
        scatter(1, 0, H, a10)
        for t in range(2):
            acc = first_product(t, H, H, f"bank{3 + t}")
            half = keep.tile([P, H], F32, name=f"a{t}1")
            nc.scalar.copy(half[:], acc[:])
            scatter(t, H, H, half)
        acc2 = first_product(2, 0, J, "bank5")
        a2 = keep.tile([P, J], F32, name="a2")
        nc.scalar.copy(a2[:], acc2[:])
        scatter(2, 0, J, a2)
        acc3 = first_product(3, 0, J, "bank6")
        a3 = shared.tile([P, J], F32, name="a3", offset=0, align_bytes=64)
        nc.scalar.copy(a3[:], acc3[:])
        scatter(3, 0, J, a3)

        g3 = keep.tile([P, 3, O], F32, name="g3")
        g4 = keep.tile([P, 3, O], F32, name="g4")
        diff = keep.tile([P, PACK, O], F32, name="diff")
        h_il = keep.tile([P, O, PACK], BF16, name="h_il", align_bytes=64)

        def fetch_pw(t, first_out, second_out):
            nc.scalar.activation(out=first_out, in_=pw[t][:].indirect(l3[:]), func=COPY, scale=sa_sb[:, t : t + 1])
            nc.scalar.activation(out=second_out, in_=pw[t][:].indirect(l4[:]), func=COPY, scale=sb_sb[:, t : t + 1])

        def magnitude(t, cols):
            nc.scalar.activation(
                out=h_il[:, cols, t : t + 2], in_=diff[:, t : t + 2, cols].rearrange("p t o -> p o t"), func=ABS
            )

        for t in range(2):
            fetch_pw(t, g3[:, t, :], g4[:, t, :])
        nc.gpsimd.tensor_tensor(diff[:, 0:2, :], g3[:, 0:2, :], g4[:, 0:2, :], SUB)
        magnitude(0, slice(0, O))
        fetch_pw(2, g3[:, 2, :], g4[:, 2, :])
        nc.gpsimd.tensor_tensor(diff[:, 2, :], g3[:, 2, :], g4[:, 2, :], SUB)
        fetch_pw(3, diff[:, 0, :], diff[:, 1, :])

        xr_codes = shared.tile([P, O], U32, name="xr_codes", offset=0, align_bytes=64)
        xr_picked = shared.tile([P, O], U8, name="xr_picked", offset=4 * O, align_bytes=64)
        nc.vector.tensor_copy(xr_codes[:], xr_sb[:].indirect(l5[:]))
        nc.vector.tensor_copy(xr_picked[:], xr_plane[:].indirect(l5[:]))
        halves = [slice(v * V, (v + 1) * V) for v in range(2)]
        p_acc = {}
        for v in range(2):
            for i in range(2):
                p_acc[i, v] = psum.tile([P, V], F32, name=f"p_acc{i}{v}", tag=f"bank{2 * v + i}")
                nc.tensor.matmul_mx(
                    out=p_acc[i, v][:],
                    lhsT=ws_sb[:, 2 * P * i : 2 * P * (i + 1)].bitcast(FP4X4),
                    lhsT_scale=ws_plane[:, P * i : P * (i + 1)],
                    rhs=xr_codes[:, halves[v]].bitcast(FP8X4),
                    rhs_scale=xr_picked[:, halves[v]],
                    start=True,
                    stop=False,
                )

        h_codes = keep.tile([P, O], U32, name="h_codes", align_bytes=64)
        h_plane = keep.tile([P, O], U8, name="h_plane", align_bytes=64)
        p_sb = [keep.tile([P, O], F32, name=f"p_sb{i}") for i in range(2)]
        for v in range(2):
            nc.vector.tensor_tensor(diff[:, 3, halves[v]], diff[:, 0, halves[v]], diff[:, 1, halves[v]], SUB)
        for v in range(2):
            magnitude(2, halves[v])
        for v in range(2):
            nc.vector.quantize_mx(
                out=h_codes[:, halves[v]].bitcast(FP8X4),
                scales=h_plane[:, halves[v]],
                in_=h_il[:, halves[v], :].rearrange("p o t -> p (o t)"),
            )
        for v in range(2):
            for i in range(2):
                nc.tensor.matmul_mx(
                    out=p_acc[i, v][:],
                    lhsT=wb_sb[:, P * i : P * (i + 1)].bitcast(FP8X4),
                    lhsT_scale=wb_plane[:, P * i : P * (i + 1)],
                    rhs=h_codes[:, halves[v]].bitcast(FP8X4),
                    rhs_scale=h_plane[:, halves[v]],
                    start=False,
                    stop=True,
                )
        for i in range(2):
            nc.scalar.copy(p_sb[i][:, halves[0]], p_acc[i, 0][:])
        for i in range(2):
            nc.vector.tensor_copy(p_sb[i][:, halves[1]], p_acc[i, 1][:])
        for i in range(2):
            first = keep.tile([P, U], F32, name=f"first{i}")
            second = keep.tile([P, U], F32, name=f"second{i}")
            nc.scalar.activation(out=first[:], in_=p_sb[i][:].indirect(l6[:]), func=COPY, scale=so_sb[:, i : i + 1])
            nc.scalar.activation(out=second[:], in_=p_sb[i][:].indirect(l7[:]), func=COPY, scale=sp_sb[:, i : i + 1])
            res = keep.tile([P, U], F32, name=f"res{i}")
            nc.vector.tensor_tensor(res[:], first[:], second[:], SUB)
            nc.sync.dma_start(out[P * i : P * (i + 1), :], res[:])
